import numpy as np
import ml_dtypes


def mxq(x, axis, fmt="e4m3"):
    dtype, down = {"e4m3": (ml_dtypes.float8_e4m3fn, 7), "e5m2": (ml_dtypes.float8_e5m2, 14)}[fmt]
    v = np.moveaxis(np.asarray(x, np.float32).astype(ml_dtypes.bfloat16).astype(np.float64), axis, -1)
    blocks = v.reshape(v.shape[:-1] + (-1, 32))
    amax = np.abs(blocks).max(-1, keepdims=True)
    byte = np.maximum(np.where(amax > 0, np.frexp(amax)[1] - 1 + 127, 0) - down, 1)
    scale = np.exp2(byte - 127.0)
    codes = (blocks / scale).astype(np.float32).astype(dtype).astype(np.float64)
    return np.moveaxis((codes * scale).reshape(v.shape), -1, axis)


WIDE = False


def mx_kscale(k):
    if not WIDE:
        return np.ones(k)
    levels = np.array([10, -10, 5, -5, 0])
    if k % 512:
        return np.exp2(np.random.permutation(np.resize(levels, k // 32))).repeat(32)
    a = np.empty((k // 512, 16))
    for p in range(k // 512):
        a[p, :8] = np.random.permutation(np.resize(levels, 8))
        for g in range(8):
            far = levels[np.abs(levels - a[p, g]) >= 10]
            a[p, g + 8] = far[np.random.randint(len(far))]
    return np.exp2(a.ravel()).repeat(32)


def f64(x):
    return np.asarray(x).astype(np.float64)


def striped(idx):
    return np.tile(idx.reshape(-1, 16).T, (8, 1)).astype(np.uint16)


def unstriped(offs):
    return offs[:16].T.reshape(-1).astype(np.int64)


E2M1 = np.array([0.0, 0.5, 1.0, 1.5, 2.0, 3.0, 4.0, 6.0, -0.0, -0.5, -1.0, -1.5, -2.0, -3.0, -4.0, -6.0])


def pack_weight(w, fmt):
    k, n = w.shape
    w = f64(np.asarray(w, np.float32).astype(ml_dtypes.bfloat16)).reshape(k // 32, 32, n)
    amax = np.abs(w).max(1)
    if fmt == "e4m3":
        byte = np.frexp(amax)[1] - 1 + 127 - 7
    else:
        mant, ex = np.frexp(amax / 6.0)
        byte = np.where(mant > 0.5, ex, ex - 1) + 127
    byte = np.clip(np.where(amax > 0, byte, 1), 1, 254)
    scaled = (w * np.exp2(127.0 - byte)[:, None, :]).reshape(k, n).astype(np.float32)
    by_word = np.ascontiguousarray(scaled.reshape(k // 512, 128, 4, n).transpose(0, 1, 3, 2))
    if fmt == "e4m3":
        words = by_word.astype(ml_dtypes.float8_e4m3fn).view(np.uint8)
    else:
        c = by_word.astype(ml_dtypes.float4_e2m1fn).view(np.uint8) & 0xF
        words = (c[..., 0::2] | (c[..., 1::2] << 4)).reshape(k // 512, 128, 2 * n)
    return np.ascontiguousarray(words), np.ascontiguousarray(byte.astype(np.uint8).reshape(k // 512, 16, n))


def unpack_weight(words, scales, fmt):
    g, _, n = scales.shape
    words = np.ascontiguousarray(words).reshape(g, 128, n, -1)
    if fmt == "e4m3":
        vals = words.view(ml_dtypes.float8_e4m3fn).astype(np.float64)
    else:
        nib = np.empty((g, 128, n, 4), np.uint8)
        nib[..., 0::2] = words & 0xF
        nib[..., 1::2] = words >> 4
        vals = E2M1[nib]
    vals = vals * np.repeat(np.exp2(scales.astype(np.float64) - 127.0), 8, axis=1)[..., None]
    return vals.transpose(0, 1, 3, 2).reshape(g * 512, n)


def relu2(v):
    return np.maximum(v, 0.0) ** 2


K, T, E, C, H, N = 1024, 2048, 8, 128, 512, 128


def by_expert(wq, xq):
    return np.concatenate([wq[e].T @ xq[:, e * C:(e + 1) * C] for e in range(E)], axis=1)


def setup_inputs():
    n = np.random.standard_normal
    s = mx_kscale(K)[:, None]
    u = mx_kscale(H)
    w1 = [pack_weight(m, "e2m1") for m in n((E, K, H)) / np.sqrt(K) / s[None] * u[None, None, :]]
    w2 = [pack_weight(m, "e2m1") for m in n((E, H, N)) / np.sqrt(H) / u[None, :, None] ** 2]
    return {
        "xT": (n((K, T)) * s).astype(np.float32),
        "w1_words": np.stack([m[0] for m in w1]),
        "w1_scales": np.stack([m[1] for m in w1]),
        "w2_words": np.stack([m[0] for m in w2]),
        "w2_scales": np.stack([m[1] for m in w2]),
        "gate": np.tile(np.random.uniform(0.2, 1.0, E * C), (N, 1)).astype(np.float32),
        "offs": striped(np.random.permutation(T)[:E * C]),
    }


def reference(xT, w1_words, w1_scales, w2_words, w2_scales, gate, offs):
    idx = unstriped(offs)
    w1 = np.stack([unpack_weight(w1_words[e], w1_scales[e], "e2m1") for e in range(E)])
    w2 = np.stack([unpack_weight(w2_words[e], w2_scales[e], "e2m1") for e in range(E)])
    xq = mxq(f64(xT)[:, idx], 0, "e4m3")
    h = relu2(by_expert(w1, xq))
    y = by_expert(w2, mxq(h, 0, "e4m3"))
    out = np.zeros((N, T))
    out[:, idx] = f64(gate) * y
    return out

@@ -1,0 +1,203 @@
+from contextlib import ExitStack
+
+import concourse.mybir as mybir
+from concourse.masks import make_identity
+
+K, T, E, C, H, N = 1024, 2048, 8, 128, 512, 128
+SLOTS = E * C
+FLOPS = 2 * SLOTS * (K * H + H * N)
+
+F32 = mybir.dt.float32
+BF16 = mybir.dt.bfloat16
+I32 = mybir.dt.int32
+U32 = mybir.dt.uint32
+U16 = mybir.dt.uint16
+U8 = mybir.dt.uint8
+FP8X4 = mybir.dt.float8_e4m3fn_x4
+FP4X4 = mybir.dt.float4_e2m1fn_x4
+ACT = mybir.ActivationFunctionType
+MULT = mybir.AluOpType.mult
+
+P = 128
+PASSES = K // 512
+GROUP = 256
+GROUPS = SLOTS // GROUP
+
+CHUNKS = (
+    (0, 0, 256, 128),
+    (0, 256, 256, 96),
+    (0, 512, 512, 192),
+    (0, 1024, 512, 192),
+    (0, 1536, 512, 192),
+    (1, 0, 512, 64),
+    (1, 512, 512, 64),
+    (1, 1024, 512, 96),
+    (1, 1536, 256, 96),
+    (1, 1792, 256, 160),
+)
+
+
+def tile_moe_pln_mlp_relu2_kernel(tc, xT, w1_words, w1_scales, w2_words, w2_scales, gate, offs, out):
+    nc = tc.nc
+    with ExitStack() as ctx:
+        lists = ctx.enter_context(tc.tile_pool(name="lists", bufs=1))
+        held = ctx.enter_context(tc.tile_pool(name="held", bufs=1))
+        psum_v = ctx.enter_context(tc.psum_pool(name="psum_v", bufs=3))
+        psum_t = ctx.enter_context(tc.psum_pool(name="psum_t", bufs=3))
+        psum_y = ctx.enter_context(tc.psum_pool(name="psum_y", bufs=2))
+
+        offsets = lists.tile([P, SLOTS // 16], U16, name="offsets")
+        nc.sync.dma_start(offsets[:], offs)
+
+        raws = []
+        for i, (s, t0, width, by_vector) in enumerate(CHUNKS):
+            raw = held.tile([P, 4, width], F32, name=f"raw{i}")
+            nc.sync.dma_start(out=raw[:], in_=xT[512 * s : 512 * (s + 1), t0 : t0 + width].rearrange("(p j) w -> p j w", j=4))
+            raws.append(raw)
+
+        w1s = held.tile([P, E * PASSES * H], U8, name="w1s", align_bytes=64)
+        w2s = held.tile([P, E * N], U8, name="w2s", align_bytes=64)
+        out_sb = held.tile([P, T], F32, name="out_sb", align_bytes=64)
+        nc.vector.memset(w1s[:].bitcast(I32), 0)
+        nc.vector.memset(out_sb[:], 0.0)
+        bytes_all = [held.tile([P, T], U8, name=f"bytes_all{s}", align_bytes=64) for s in range(PASSES)]
+        nc.gpsimd.memset(bytes_all[0][:], 0)
+        nc.gpsimd.memset(w2s[:].bitcast(I32), 0)
+        ident = held.tile([P, P], F32, name="ident")
+        make_identity(nc, ident[:])
+        nc.gpsimd.memset(bytes_all[1][:], 0)
+        warm = held.tile([P, 1], F32, name="warm")
+        warm_in = held.tile([P, 1], F32, name="warm_in")
+        nc.vector.memset(warm_in[:], 0.0)
+        nc.scalar.activation(out=warm[:], in_=warm_in[:], func=ACT.Square)
+
+        w1w = [held.tile([P, 2 * PASSES * 2 * H], U8, name=f"w1w{g}", align_bytes=64) for g in range(GROUPS)]
+        w2w = held.tile([P, E * 2 * N], U8, name="w2w", align_bytes=64)
+        gate_sb = held.tile([P, SLOTS], F32, name="gate_sb", align_bytes=64)
+
+        w1_int = w1_words.bitcast(I32).rearrange("(g e) s p b -> g p (e s) b", e=2)
+        w1s_int = w1_scales.bitcast(I32).rearrange("e s (q r) b -> r q (e s) b", r=4)
+        w2s_int = w2_scales.bitcast(I32).rearrange("e o (q r) b -> r q (e o) b", r=4)
+
+        def load_w1(g):
+            nc.sync.dma_start(out=w1w[g][:].bitcast(I32).rearrange("p (e b) -> p e b", e=2 * PASSES), in_=w1_int[g])
+
+        load_w1(0)
+        w1s_view = w1s[:].bitcast(I32).rearrange("p (e b) -> p e b", e=E * PASSES)
+        for r in range(4):
+            nc.sync.dma_start(out=w1s_view[r:P:32], in_=w1s_int[r])
+        load_w1(1)
+        nc.sync.dma_start(
+            out=w2w[:].bitcast(I32).rearrange("p (e b) -> p e b", e=E),
+            in_=w2_words.bitcast(I32).rearrange("e o p b -> p (e o) b"),
+        )
+        w2s_view = w2s[:].bitcast(I32).rearrange("p (e b) -> p e b", e=E)
+        for r in range(4):
+            nc.sync.dma_start(out=w2s_view[r:P:32], in_=w2s_int[r])
+        nc.sync.dma_start(out=gate_sb[:], in_=gate)
+        load_w1(2)
+        load_w1(3)
+
+        words_all = [held.tile([P, T], U32, name=f"words_all{s}", align_bytes=64) for s in range(PASSES)]
+        words = [held.tile([P, SLOTS], U32, name=f"words{s}", align_bytes=64) for s in range(PASSES)]
+        scales = [held.tile([P, SLOTS], U8, name=f"scales{s}", align_bytes=64) for s in range(PASSES)]
+
+        def gather(s, a, b):
+            picked = offsets[:, a // 16 : b // 16]
+            nc.vector.tensor_copy(words[s][:, a:b], words_all[s][:].indirect(picked))
+            nc.vector.tensor_copy(scales[s][:, a:b], bytes_all[s][:].indirect(picked))
+
+        for i, (s, t0, width, by_vector) in enumerate(CHUNKS):
+            piece = held.tile([P, width, 4], BF16, name=f"piece{i}", align_bytes=64)
+            for a, b, mover in ((0, by_vector, "v"), (by_vector, width, "s")):
+                if a == b:
+                    continue
+                dst = piece[:, a:b, :].rearrange("p (c i) t -> p c t i", i=4)
+                src = raws[i][:, :, a:b].rearrange("p t (c i) -> p c t i", i=4)
+                if mover == "v":
+                    nc.vector.tensor_copy(dst, src)
+                else:
+                    nc.scalar.activation(out=dst, in_=src, func=ACT.Copy)
+            nc.vector.quantize_mx(
+                out=words_all[s][:, t0 : t0 + width].bitcast(FP8X4),
+                scales=bytes_all[s][:, t0 : t0 + width],
+                in_=piece[:].rearrange("p w t -> p (w t)"),
+            )
+            if s == 0 and t0 + width == T:
+                gather(0, 0, SLOTS)
+
+        for a, b in ((0, 256), (256, 512), (512, 1024)):
+            gather(PASSES - 1, a, b)
+
+        y_sb = held.tile([P, SLOTS], F32, name="y_sb", align_bytes=64)
+        v, r, turned, h, h_words, h_scales, y = {}, {}, {}, {}, {}, {}, {}
+
+        def first_layer(e):
+            g, half = divmod(e, 2)
+            slots = slice(e * C, (e + 1) * C)
+            v[e] = psum_v.tile([C, H], F32, name="v")
+            for s in range(PASSES):
+                at = (half * PASSES + s) * 2 * H
+                sc = (e * PASSES + s) * H
+                nc.tensor.matmul_mx(
+                    out=v[e][:],
+                    lhsT=words[s][:, slots].bitcast(FP8X4),
+                    lhsT_scale=scales[s][:, slots],
+                    rhs=w1w[g][:, at : at + 2 * H].bitcast(FP4X4),
+                    rhs_scale=w1s[:, sc : sc + H],
+                    start=(s == 0),
+                    stop=(s == PASSES - 1),
+                )
+
+        def relu(e):
+            r[e] = held.tile([C, 4, P], F32, name=f"r{e}")
+            nc.scalar.activation(out=r[e][:], in_=v[e][:].rearrange("c (p t) -> c t p", t=4), func=ACT.Relu)
+
+        def turn(e):
+            turned[e] = psum_t.tile([P, 4, C], F32, name="turned")
+            for t in range(4):
+                nc.tensor.transpose(turned[e][:, t, :], r[e][:, t, :], ident[:])
+
+        def square(e):
+            h[e] = held.tile([P, C, 4], BF16, name=f"h{e}", align_bytes=64)
+            nc.scalar.activation(out=h[e][:], in_=turned[e][:].rearrange("p t c -> p c t"), func=ACT.Square)
+
+        def quantise(e):
+            h_words[e] = held.tile([P, C], U32, name=f"h_words{e}", align_bytes=64)
+            h_scales[e] = held.tile([P, C], U8, name=f"h_scales{e}", align_bytes=64)
+            nc.vector.quantize_mx(out=h_words[e][:].bitcast(FP8X4), scales=h_scales[e][:], in_=h[e][:].rearrange("p c t -> p (c t)"))
+
+        def second_layer(e):
+            g, half = divmod(e, 2)
+            if half == 0:
+                y[g] = psum_y.tile([N, 2 * C], F32, name="y")
+            nc.tensor.matmul_mx(
+                out=y[g][:, half * C : (half + 1) * C],
+                lhsT=w2w[:, e * 2 * N : (e + 1) * 2 * N].bitcast(FP4X4),
+                lhsT_scale=w2s[:, e * N : (e + 1) * N],
+                rhs=h_words[e][:].bitcast(FP8X4),
+                rhs_scale=h_scales[e][:],
+                start=True,
+                stop=True,
+            )
+
+        def put_back(g):
+            cols = slice(g * GROUP, (g + 1) * GROUP)
+            nc.scalar.copy(y_sb[:, cols], y[g][:])
+            picked = offsets[:, g * GROUP // 16 : (g + 1) * GROUP // 16]
+            nc.vector.tensor_tensor(out_sb[:].indirect(picked), y_sb[:, cols], gate_sb[:, cols], MULT)
+
+        for k in range(E + 3):
+            if k < E:
+                first_layer(k)
+                relu(k)
+            if 0 <= k - 1 < E:
+                turn(k - 1)
+                square(k - 1)
+            if 0 <= k - 2 < E:
+                quantise(k - 2)
+            if 0 <= k - 3 < E:
+                second_layer(k - 3)
+                if k % 2 == 0:
+                    put_back((k - 3) // 2)
+        nc.sync.dma_start(out=out, in_=out_sb[:])

@@ -22,6 +22,7 @@ P = 128
 PASSES = K // 512
 GROUP = 256
 GROUPS = SLOTS // GROUP
+FIRST = 4
 
 CHUNKS = (
     (0, 0, 256, 128),
@@ -47,13 +48,14 @@ def tile_moe_pln_mlp_relu2_kernel(tc, xT, w1_words, w1_scales, w2_words, w2_scal
         psum_y = ctx.enter_context(tc.psum_pool(name="psum_y", bufs=2))
 
         offsets = lists.tile([P, SLOTS // 16], U16, name="offsets")
-        nc.sync.dma_start(offsets[:], offs)
 
         raws = []
         for i, (s, t0, width, by_vector) in enumerate(CHUNKS):
             raw = held.tile([P, 4, width], F32, name=f"raw{i}")
             nc.sync.dma_start(out=raw[:], in_=xT[512 * s : 512 * (s + 1), t0 : t0 + width].rearrange("(p j) w -> p j w", j=4))
             raws.append(raw)
+            if i == 0:
+                nc.sync.dma_start(offsets[:], offs)
 
         w1s = held.tile([P, E * PASSES * H], U8, name="w1s", align_bytes=64)
         w2s = held.tile([P, E * N], U8, name="w2s", align_bytes=64)
@@ -82,10 +84,15 @@ def tile_moe_pln_mlp_relu2_kernel(tc, xT, w1_words, w1_scales, w2_words, w2_scal
         def load_w1(g):
             nc.sync.dma_start(out=w1w[g][:].bitcast(I32).rearrange("p (e b) -> p e b", e=2 * PASSES), in_=w1_int[g])
 
-        load_w1(0)
         w1s_view = w1s[:].bitcast(I32).rearrange("p (e b) -> p e b", e=E * PASSES)
-        for r in range(4):
-            nc.sync.dma_start(out=w1s_view[r:P:32], in_=w1s_int[r])
+
+        def load_w1_scales(a, b):
+            for r in range(4):
+                nc.sync.dma_start(out=w1s_view[r:P:32, a:b, :], in_=w1s_int[r][:, a:b, :])
+
+        load_w1_scales(0, FIRST)
+        load_w1(0)
+        load_w1_scales(FIRST, E * PASSES)
         load_w1(1)
         nc.sync.dma_start(
             out=w2w[:].bitcast(I32).rearrange("p (e b) -> p e b", e=E),

from contextlib import ExitStack

import concourse.mybir as mybir
from concourse.masks import make_identity

K, T, E, C, H, N = 1024, 2048, 8, 128, 512, 128
SLOTS = E * C
FLOPS = 2 * SLOTS * (K * H + H * N)

F32 = mybir.dt.float32
BF16 = mybir.dt.bfloat16
I32 = mybir.dt.int32
U32 = mybir.dt.uint32
U16 = mybir.dt.uint16
U8 = mybir.dt.uint8
FP8X4 = mybir.dt.float8_e4m3fn_x4
FP4X4 = mybir.dt.float4_e2m1fn_x4
ACT = mybir.ActivationFunctionType
MULT = mybir.AluOpType.mult

P = 128
PASSES = K // 512
GROUP = 256
GROUPS = SLOTS // GROUP
FIRST = 4

CHUNKS = (
    (0, 0, 256, 128),
    (0, 256, 256, 96),
    (0, 512, 512, 192),
    (0, 1024, 512, 192),
    (0, 1536, 512, 192),
    (1, 0, 512, 64),
    (1, 512, 512, 64),
    (1, 1024, 512, 96),
    (1, 1536, 256, 96),
    (1, 1792, 256, 160),
)


def tile_moe_pln_mlp_relu2_kernel(tc, xT, w1_words, w1_scales, w2_words, w2_scales, gate, offs, out):
    nc = tc.nc
    with ExitStack() as ctx:
        lists = ctx.enter_context(tc.tile_pool(name="lists", bufs=1))
        held = ctx.enter_context(tc.tile_pool(name="held", bufs=1))
        psum_v = ctx.enter_context(tc.psum_pool(name="psum_v", bufs=3))
        psum_t = ctx.enter_context(tc.psum_pool(name="psum_t", bufs=3))
        psum_y = ctx.enter_context(tc.psum_pool(name="psum_y", bufs=2))

        offsets = lists.tile([P, SLOTS // 16], U16, name="offsets")

        raws = []
        for i, (s, t0, width, by_vector) in enumerate(CHUNKS):
            raw = held.tile([P, 4, width], F32, name=f"raw{i}")
            nc.sync.dma_start(out=raw[:], in_=xT[512 * s : 512 * (s + 1), t0 : t0 + width].rearrange("(p j) w -> p j w", j=4))
            raws.append(raw)
            if i == 0:
                nc.sync.dma_start(offsets[:], offs)

        w1s = held.tile([P, E * PASSES * H], U8, name="w1s", align_bytes=64)
        w2s = held.tile([P, E * N], U8, name="w2s", align_bytes=64)
        out_sb = held.tile([P, T], F32, name="out_sb", align_bytes=64)
        nc.vector.memset(w1s[:].bitcast(I32), 0)
        nc.vector.memset(out_sb[:], 0.0)
        bytes_all = [held.tile([P, T], U8, name=f"bytes_all{s}", align_bytes=64) for s in range(PASSES)]
        nc.gpsimd.memset(bytes_all[0][:], 0)
        nc.gpsimd.memset(w2s[:].bitcast(I32), 0)
        ident = held.tile([P, P], F32, name="ident")
        make_identity(nc, ident[:])
        nc.gpsimd.memset(bytes_all[1][:], 0)
        warm = held.tile([P, 1], F32, name="warm")
        warm_in = held.tile([P, 1], F32, name="warm_in")
        nc.vector.memset(warm_in[:], 0.0)
        nc.scalar.activation(out=warm[:], in_=warm_in[:], func=ACT.Square)

        w1w = [held.tile([P, 2 * PASSES * 2 * H], U8, name=f"w1w{g}", align_bytes=64) for g in range(GROUPS)]
        w2w = held.tile([P, E * 2 * N], U8, name="w2w", align_bytes=64)
        gate_sb = held.tile([P, SLOTS], F32, name="gate_sb", align_bytes=64)

        w1_int = w1_words.bitcast(I32).rearrange("(g e) s p b -> g p (e s) b", e=2)
        w1s_int = w1_scales.bitcast(I32).rearrange("e s (q r) b -> r q (e s) b", r=4)
        w2s_int = w2_scales.bitcast(I32).rearrange("e o (q r) b -> r q (e o) b", r=4)

        def load_w1(g):
            nc.sync.dma_start(out=w1w[g][:].bitcast(I32).rearrange("p (e b) -> p e b", e=2 * PASSES), in_=w1_int[g])

        w1s_view = w1s[:].bitcast(I32).rearrange("p (e b) -> p e b", e=E * PASSES)

        def load_w1_scales(a, b):
            for r in range(4):
                nc.sync.dma_start(out=w1s_view[r:P:32, a:b, :], in_=w1s_int[r][:, a:b, :])

        load_w1_scales(0, FIRST)
        load_w1(0)
        load_w1_scales(FIRST, E * PASSES)
        load_w1(1)
        nc.sync.dma_start(
            out=w2w[:].bitcast(I32).rearrange("p (e b) -> p e b", e=E),
            in_=w2_words.bitcast(I32).rearrange("e o p b -> p (e o) b"),
        )
        w2s_view = w2s[:].bitcast(I32).rearrange("p (e b) -> p e b", e=E)
        for r in range(4):
            nc.sync.dma_start(out=w2s_view[r:P:32], in_=w2s_int[r])
        nc.sync.dma_start(out=gate_sb[:], in_=gate)
        load_w1(2)
        load_w1(3)

        words_all = [held.tile([P, T], U32, name=f"words_all{s}", align_bytes=64) for s in range(PASSES)]
        words = [held.tile([P, SLOTS], U32, name=f"words{s}", align_bytes=64) for s in range(PASSES)]
        scales = [held.tile([P, SLOTS], U8, name=f"scales{s}", align_bytes=64) for s in range(PASSES)]

        def gather(s, a, b):
            picked = offsets[:, a // 16 : b // 16]
            nc.vector.tensor_copy(words[s][:, a:b], words_all[s][:].indirect(picked))
            nc.vector.tensor_copy(scales[s][:, a:b], bytes_all[s][:].indirect(picked))

        for i, (s, t0, width, by_vector) in enumerate(CHUNKS):
            piece = held.tile([P, width, 4], BF16, name=f"piece{i}", align_bytes=64)
            for a, b, mover in ((0, by_vector, "v"), (by_vector, width, "s")):
                if a == b:
                    continue
                dst = piece[:, a:b, :].rearrange("p (c i) t -> p c t i", i=4)
                src = raws[i][:, :, a:b].rearrange("p t (c i) -> p c t i", i=4)
                if mover == "v":
                    nc.vector.tensor_copy(dst, src)
                else:
                    nc.scalar.activation(out=dst, in_=src, func=ACT.Copy)
            nc.vector.quantize_mx(
                out=words_all[s][:, t0 : t0 + width].bitcast(FP8X4),
                scales=bytes_all[s][:, t0 : t0 + width],
                in_=piece[:].rearrange("p w t -> p (w t)"),
            )
            if s == 0 and t0 + width == T:
                gather(0, 0, SLOTS)

        for a, b in ((0, 256), (256, 512), (512, 1024)):
            gather(PASSES - 1, a, b)

        y_sb = held.tile([P, SLOTS], F32, name="y_sb", align_bytes=64)
        v, r, turned, h, h_words, h_scales, y = {}, {}, {}, {}, {}, {}, {}

        def first_layer(e):
            g, half = divmod(e, 2)
            slots = slice(e * C, (e + 1) * C)
            v[e] = psum_v.tile([C, H], F32, name="v")
            for s in range(PASSES):
                at = (half * PASSES + s) * 2 * H
                sc = (e * PASSES + s) * H
                nc.tensor.matmul_mx(
                    out=v[e][:],
                    lhsT=words[s][:, slots].bitcast(FP8X4),
                    lhsT_scale=scales[s][:, slots],
                    rhs=w1w[g][:, at : at + 2 * H].bitcast(FP4X4),
                    rhs_scale=w1s[:, sc : sc + H],
                    start=(s == 0),
                    stop=(s == PASSES - 1),
                )

        def relu(e):
            r[e] = held.tile([C, 4, P], F32, name=f"r{e}")
            nc.scalar.activation(out=r[e][:], in_=v[e][:].rearrange("c (p t) -> c t p", t=4), func=ACT.Relu)

        def turn(e):
            turned[e] = psum_t.tile([P, 4, C], F32, name="turned")
            for t in range(4):
                nc.tensor.transpose(turned[e][:, t, :], r[e][:, t, :], ident[:])

        def square(e):
            h[e] = held.tile([P, C, 4], BF16, name=f"h{e}", align_bytes=64)
            nc.scalar.activation(out=h[e][:], in_=turned[e][:].rearrange("p t c -> p c t"), func=ACT.Square)

        def quantise(e):
            h_words[e] = held.tile([P, C], U32, name=f"h_words{e}", align_bytes=64)
            h_scales[e] = held.tile([P, C], U8, name=f"h_scales{e}", align_bytes=64)
            nc.vector.quantize_mx(out=h_words[e][:].bitcast(FP8X4), scales=h_scales[e][:], in_=h[e][:].rearrange("p c t -> p (c t)"))

        def second_layer(e):
            g, half = divmod(e, 2)
            if half == 0:
                y[g] = psum_y.tile([N, 2 * C], F32, name="y")
            nc.tensor.matmul_mx(
                out=y[g][:, half * C : (half + 1) * C],
                lhsT=w2w[:, e * 2 * N : (e + 1) * 2 * N].bitcast(FP4X4),
                lhsT_scale=w2s[:, e * N : (e + 1) * N],
                rhs=h_words[e][:].bitcast(FP8X4),
                rhs_scale=h_scales[e][:],
                start=True,
                stop=True,
            )

        def put_back(g):
            cols = slice(g * GROUP, (g + 1) * GROUP)
            nc.scalar.copy(y_sb[:, cols], y[g][:])
            picked = offsets[:, g * GROUP // 16 : (g + 1) * GROUP // 16]
            nc.vector.tensor_tensor(out_sb[:].indirect(picked), y_sb[:, cols], gate_sb[:, cols], MULT)

        for k in range(E + 3):
            if k < E:
                first_layer(k)
                relu(k)
            if 0 <= k - 1 < E:
                turn(k - 1)
                square(k - 1)
            if 0 <= k - 2 < E:
                quantise(k - 2)
            if 0 <= k - 3 < E:
                second_layer(k - 3)
                if k % 2 == 0:
                    put_back((k - 3) // 2)
        nc.sync.dma_start(out=out, in_=out_sb[:])
